import numpy as np
import ml_dtypes


def mxq(x, axis, fmt="e4m3"):
    dtype, down = {"e4m3": (ml_dtypes.float8_e4m3fn, 7), "e5m2": (ml_dtypes.float8_e5m2, 14)}[fmt]
    v = np.moveaxis(np.asarray(x, np.float32).astype(ml_dtypes.bfloat16).astype(np.float64), axis, -1)
    blocks = v.reshape(v.shape[:-1] + (-1, 32))
    amax = np.abs(blocks).max(-1, keepdims=True)
    byte = np.maximum(np.where(amax > 0, np.frexp(amax)[1] - 1 + 127, 0) - down, 1)
    scale = np.exp2(byte - 127.0)
    codes = (blocks / scale).astype(np.float32).astype(dtype).astype(np.float64)
    return np.moveaxis((codes * scale).reshape(v.shape), -1, axis)


WIDE = False


def mx_kscale(k):
    if not WIDE:
        return np.ones(k)
    levels = np.array([10, -10, 5, -5, 0])
    if k % 512:
        return np.exp2(np.random.permutation(np.resize(levels, k // 32))).repeat(32)
    a = np.empty((k // 512, 16))
    for p in range(k // 512):
        a[p, :8] = np.random.permutation(np.resize(levels, 8))
        for g in range(8):
            far = levels[np.abs(levels - a[p, g]) >= 10]
            a[p, g + 8] = far[np.random.randint(len(far))]
    return np.exp2(a.ravel()).repeat(32)


def f64(x):
    return np.asarray(x).astype(np.float64)


def striped(idx):
    return np.tile(idx.reshape(-1, 16).T, (8, 1)).astype(np.uint16)


def unstriped(offs):
    return offs[:16].T.reshape(-1).astype(np.int64)


E2M1 = np.array([0.0, 0.5, 1.0, 1.5, 2.0, 3.0, 4.0, 6.0, -0.0, -0.5, -1.0, -1.5, -2.0, -3.0, -4.0, -6.0])


def pack_weight(w, fmt):
    k, n = w.shape
    w = f64(np.asarray(w, np.float32).astype(ml_dtypes.bfloat16)).reshape(k // 32, 32, n)
    amax = np.abs(w).max(1)
    if fmt == "e4m3":
        byte = np.frexp(amax)[1] - 1 + 127 - 7
    else:
        mant, ex = np.frexp(amax / 6.0)
        byte = np.where(mant > 0.5, ex, ex - 1) + 127
    byte = np.clip(np.where(amax > 0, byte, 1), 1, 254)
    scaled = (w * np.exp2(127.0 - byte)[:, None, :]).reshape(k, n).astype(np.float32)
    by_word = np.ascontiguousarray(scaled.reshape(k // 512, 128, 4, n).transpose(0, 1, 3, 2))
    if fmt == "e4m3":
        words = by_word.astype(ml_dtypes.float8_e4m3fn).view(np.uint8)
    else:
        c = by_word.astype(ml_dtypes.float4_e2m1fn).view(np.uint8) & 0xF
        words = (c[..., 0::2] | (c[..., 1::2] << 4)).reshape(k // 512, 128, 2 * n)
    return np.ascontiguousarray(words), np.ascontiguousarray(byte.astype(np.uint8).reshape(k // 512, 16, n))


def unpack_weight(words, scales, fmt):
    g, _, n = scales.shape
    words = np.ascontiguousarray(words).reshape(g, 128, n, -1)
    if fmt == "e4m3":
        vals = words.view(ml_dtypes.float8_e4m3fn).astype(np.float64)
    else:
        nib = np.empty((g, 128, n, 4), np.uint8)
        nib[..., 0::2] = words & 0xF
        nib[..., 1::2] = words >> 4
        vals = E2M1[nib]
    vals = vals * np.repeat(np.exp2(scales.astype(np.float64) - 127.0), 8, axis=1)[..., None]
    return vals.transpose(0, 1, 3, 2).reshape(g * 512, n)


def sigmoid(v):
    return 1.0 / (1.0 + np.exp(-np.maximum(v, -700.0)))


def d_sigmoid(v):
    s = 1.0 / (1.0 + np.exp(-np.maximum(v, -700.0)))
    return s * (1.0 - s)


K, T, E, C, H, N = 128, 768, 2, 256, 1024, 1536


def by_expert(wq, xq):
    return np.concatenate([wq[e].T @ xq[:, e * C:(e + 1) * C] for e in range(E)], axis=1)


def setup_inputs():
    n = np.random.standard_normal
    s = mx_kscale(N)[:, None]
    u = mx_kscale(H)
    dy = pack_weight(n((N, T)) * s, "e4m3")
    w2 = [pack_weight(m, "e2m1") for m in n((E, N, H)) / np.sqrt(N) / s[None] * u[None, None, :]]
    w1 = [pack_weight(m, "e2m1") for m in n((E, H, K)) / np.sqrt(H) / u[None, :, None]]
    w3 = [pack_weight(m, "e2m1") for m in n((E, H, K)) / np.sqrt(H) / u[None, :, None]]
    return {
        "dy_words": dy[0],
        "dy_scales": dy[1],
        "a1": n((H, E * C)).astype(np.float32),
        "a3": n((H, E * C)).astype(np.float32),
        "w2_words": np.stack([m[0] for m in w2]),
        "w2_scales": np.stack([m[1] for m in w2]),
        "w1_words": np.stack([m[0] for m in w1]),
        "w1_scales": np.stack([m[1] for m in w1]),
        "w3_words": np.stack([m[0] for m in w3]),
        "w3_scales": np.stack([m[1] for m in w3]),
        "gate": np.tile(np.random.uniform(0.2, 1.0, E * C), (H, 1)).astype(np.float32),
        "offs": striped(np.random.permutation(T)[:E * C]),
    }


def reference(dy_words, dy_scales, a1, a3, w2_words, w2_scales, w1_words, w1_scales, w3_words, w3_scales, gate, offs):
    idx = unstriped(offs)
    w2 = np.stack([unpack_weight(w2_words[e], w2_scales[e], "e2m1") for e in range(E)])
    w1 = np.stack([unpack_weight(w1_words[e], w1_scales[e], "e2m1") for e in range(E)])
    w3 = np.stack([unpack_weight(w3_words[e], w3_scales[e], "e2m1") for e in range(E)])
    gq = unpack_weight(dy_words, dy_scales, "e4m3")[:, idx]
    dh = f64(gate) * by_expert(w2, gq)
    da1 = dh * f64(a3) * d_sigmoid(f64(a1))
    da3 = dh * sigmoid(f64(a1))
    dx = by_expert(w1, mxq(da1, 0, "e4m3")) + by_expert(w3, mxq(da3, 0, "e4m3"))
    out = np.zeros((K, T))
    out[:, idx] = dx
    return out

@@ -1,0 +1,218 @@
+from contextlib import ExitStack
+
+import concourse.mybir as mybir
+from concourse.masks import make_identity
+
+K, T, E, C, H, N = 128, 768, 2, 256, 1024, 1536
+FLOPS = 2 * E * C * H * (N + 2 * K)
+BYTES = N * T + N * T // 32 + 2 * 4 * H * E * C + E * H * (N + 2 * K) * 17 // 32 + 4 * E * C + 128 * 64 + 4 * K * T
+
+F32 = mybir.dt.float32
+BF16 = mybir.dt.bfloat16
+I32 = mybir.dt.int32
+U32 = mybir.dt.uint32
+U16 = mybir.dt.uint16
+U8 = mybir.dt.uint8
+FP8X4 = mybir.dt.float8_e4m3fn_x4
+FP4X4 = mybir.dt.float4_e2m1fn_x4
+MULT = mybir.AluOpType.mult
+SIGMOID = mybir.ActivationFunctionType.Sigmoid
+
+P = 128
+KP = 512
+NP = N // KP
+HP = H // KP
+JT = E * C // P
+JE = C // P
+
+
+def tile_moe_bdx_glu_sigmoid_kernel(
+    tc, dy_words, dy_scales, a1, a3, w2_words, w2_scales, w1_words, w1_scales, w3_words, w3_scales, gate, offs, out
+):
+    nc = tc.nc
+    with ExitStack() as ctx:
+        keep = ctx.enter_context(tc.tile_pool(name="keep", bufs=1))
+        work = ctx.enter_context(tc.tile_pool(name="work", bufs=3))
+        psum = ctx.enter_context(tc.psum_pool(name="psum", bufs=2))
+
+        offsets = keep.tile([P, E * C // 16], U16, name="offsets")
+        nc.sync.dma_start(offsets[:], offs)
+
+        dys = keep.tile([P, NP * T], U8, name="dys", align_bytes=64)
+        w2s = [keep.tile([P, NP * H], U8, name="w2s%d" % e, align_bytes=64) for e in range(E)]
+        w13s = keep.tile([P, 2 * E * HP * K], U8, name="w13s", align_bytes=64)
+        nc.vector.memset(dys[:].bitcast(I32), 0)
+        for e in range(E):
+            nc.vector.memset(w2s[e][:].bitcast(I32), 0)
+        nc.vector.memset(w13s[:].bitcast(I32), 0)
+
+        warm = keep.tile([P, 1], F32, name="warm")
+        nc.vector.memset(warm[:], 0.0)
+        warm2 = keep.tile([P, 1], F32, name="warm2")
+        nc.scalar.activation(warm2[:], warm[:], SIGMOID)
+
+        ident = keep.tile([P, P], F32, name="ident")
+        make_identity(nc, ident[:])
+        result = keep.tile([P, T], F32, name="result")
+        nc.gpsimd.memset(result[:], 0.0)
+
+        gate_col = keep.tile([P, JT], F32, name="gate_col")
+        with nc.allow_non_contiguous_dma(reason="one gate a slot, slots on the partitions"):
+            nc.scalar.dma_start(gate_col[:], gate[0, :].rearrange("(j p) -> p j", p=P))
+
+        def load_scales(plane, src, blocks):
+            rows = src.rearrange("b (q r) n -> r q b n", r=4)
+            for r in range(4):
+                nc.sync.dma_start(
+                    plane[r:P:32, :].bitcast(I32).rearrange("q (b n) -> q b n", b=blocks), rows[r].bitcast(I32)
+                )
+
+        dyw = [keep.tile([P, T], U32, name="dyw%d" % o, align_bytes=64) for o in range(NP)]
+
+        def load_dy(o):
+            nc.sync.dma_start(dyw[o][:].bitcast(I32), dy_words[o].rearrange("p t d -> p (t d)").bitcast(I32))
+
+        w2w = {}
+        a1s = {}
+        a3s = {}
+
+        def load_w2(e, g):
+            w2w[e, g] = keep.tile([P, NP, 2 * KP], U8, name="w2w%d%d" % (e, g), align_bytes=64)
+            src = w2_words[e, :, :, 2 * KP * g : 2 * KP * (g + 1)].rearrange("s p b -> p s b")
+            nc.sync.dma_start(w2w[e, g][:].bitcast(I32), src.bitcast(I32))
+
+        def load_a(store, src, name, e, g):
+            store[e, g] = keep.tile([P, 4, C], F32, name="%s_%d%d" % (name, e, g))
+            rows = src[KP * g : KP * (g + 1), C * e : C * (e + 1)].rearrange("(p t) c -> p t c", t=4)
+            nc.sync.dma_start(store[e, g][:], rows)
+
+        w13w = keep.tile([P, 2, E * HP, 2 * K], U8, name="w13w", align_bytes=64)
+
+        load_dy(0)
+        load_scales(dys, dy_scales, NP)
+        load_dy(1)
+        load_dy(2)
+        load_scales(w2s[0], w2_scales[0], NP)
+        for e in range(E):
+            for g in range(HP):
+                if (e, g) == (1, 0):
+                    load_scales(w2s[1], w2_scales[1], NP)
+                load_w2(e, g)
+                load_a(a1s, a1, "a1", e, g)
+                load_a(a3s, a3, "a3", e, g)
+                if (e, g) == (0, 1):
+                    for m, (words, scales) in enumerate(((w1_words, w1_scales), (w3_words, w3_scales))):
+                        nc.sync.dma_start(w13w[:, m].bitcast(I32), words.rearrange("e s p b -> p (e s) b").bitcast(I32))
+                        half = E * HP * K
+                        load_scales(w13s[:, m * half : (m + 1) * half], scales.rearrange("e s f k -> (e s) f k"), E * HP)
+
+        gw = {}
+        gs = {}
+
+        def gather(j):
+            gw[j] = keep.tile([P, NP, P], U32, name="gw%d" % j, align_bytes=64)
+            gs[j] = keep.tile([P, NP, P], U8, name="gs%d" % j, align_bytes=64)
+            picks = offsets[:, 8 * j : 8 * (j + 1)]
+            for o in range(NP):
+                nc.vector.tensor_copy(gw[j][:, o, :], dyw[o][:].indirect(picks))
+                nc.vector.tensor_copy(gs[j][:, o, :], dys[:, T * o : T * (o + 1)].indirect(picks))
+
+        units = [(e, g, jj) for e in range(E) for g in range(HP) for jj in range(JE)]
+        sig_t = {}
+        wfac = {}
+        t3_t = {}
+        da = {}
+        codes = {}
+        cscales = {}
+
+        def stage_sigmoid(u):
+            e, g, jj = units[u]
+            cols = slice(P * jj, P * (jj + 1))
+            a1_t = psum.tile([P, 4, P], F32, name="a1_t")
+            for t in range(4):
+                nc.tensor.transpose(a1_t[:, t, :], a1s[e, g][:, t, cols], ident[:])
+            sig_t[u] = work.tile([P, 4, P], F32, name="sig_t")
+            nc.scalar.activation(sig_t[u][:], a1_t[:], SIGMOID)
+            sig_m = work.tile([P, 4, P], F32, name="sig_m")
+            nc.scalar.activation(sig_m[:], a1s[e, g][:, :, cols], SIGMOID, scale=-1.0)
+            wfac[u] = work.tile([P, 4, P], F32, name="wfac", bufs=4)
+            nc.gpsimd.tensor_tensor(wfac[u][:], sig_m[:], a3s[e, g][:, :, cols], MULT)
+
+        def stage_dh(u):
+            e, g, jj = units[u]
+            j = JE * e + jj
+            dh_t = psum.tile([P, KP], F32, name="dh_t")
+            for o in range(NP):
+                nc.tensor.matmul_mx(
+                    out=dh_t[:],
+                    lhsT=gw[j][:, o, :].bitcast(FP8X4),
+                    lhsT_scale=gs[j][:, o, :],
+                    rhs=w2w[e, g][:, o, :].bitcast(FP4X4),
+                    rhs_scale=w2s[e][:, H * o + KP * g : H * o + KP * (g + 1)],
+                    start=(o == 0),
+                    stop=(o == NP - 1),
+                )
+            t3_t[u] = work.tile([P, 4, P], F32, name="t3_t")
+            nc.vector.scalar_tensor_tensor(
+                t3_t[u][:], dh_t[:].rearrange("p (m t) -> p t m", t=4), gate_col[:, j : j + 1], sig_t[u][:], MULT, MULT
+            )
+
+        def stage_da(u):
+            t3 = psum.tile([P, 4, P], F32, name="t3", bufs=3)
+            for t in range(4):
+                nc.tensor.transpose(t3[:, t, :], t3_t[u][:, t, :], ident[:])
+            da[u] = work.tile([P, 2, P, 4], BF16, name="da", align_bytes=64)
+            nc.vector.tensor_tensor(
+                da[u][:, 0].rearrange("p (c i) t -> p c t i", i=4),
+                t3[:].rearrange("p t (c i) -> p c t i", i=4),
+                wfac[u][:].rearrange("p t (c i) -> p c t i", i=4),
+                MULT,
+            )
+            nc.scalar.copy(da[u][:, 1], t3[:].rearrange("p t n -> p n t"))
+
+        def stage_quant(u):
+            codes[u] = keep.tile([P, 2 * P], U32, name="codes%d" % u, align_bytes=64)
+            cscales[u] = keep.tile([P, 2 * P], U8, name="cscales%d" % u, align_bytes=64)
+            nc.vector.quantize_mx(
+                out=codes[u][:].bitcast(FP8X4), scales=cscales[u][:], in_=da[u][:].rearrange("p m n t -> p (m n t)")
+            )
+
+        def stage_dx(u):
+            e, g, jj = units[u]
+            j = JE * e + jj
+            dx = psum.tile([P, P], F32, name="dx", bufs=1)
+            for gg in range(HP):
+                v = units.index((e, gg, jj))
+                for m in range(2):
+                    blk = (m * E + e) * HP + gg
+                    nc.tensor.matmul_mx(
+                        out=dx[:],
+                        lhsT=w13w[:, m, e * HP + gg, :].bitcast(FP4X4),
+                        lhsT_scale=w13s[:, K * blk : K * (blk + 1)],
+                        rhs=codes[v][:, P * m : P * (m + 1)].bitcast(FP8X4),
+                        rhs_scale=cscales[v][:, P * m : P * (m + 1)],
+                        start=(gg == 0 and m == 0),
+                        stop=(gg == HP - 1 and m == 1),
+                    )
+            dx_sb = work.tile([P, P], F32, name="dx_sb")
+            nc.scalar.copy(dx_sb[:], dx[:])
+            nc.vector.tensor_copy(result[:].indirect(offsets[:, 8 * j : 8 * (j + 1)]), dx_sb[:])
+
+        gather(0)
+        gather(1)
+        stage_sigmoid(0)
+        count = len(units)
+        for step in range(count + 2):
+            if step + 1 < count:
+                stage_sigmoid(step + 1)
+            if step < count:
+                stage_dh(step)
+            if 0 <= step - 1 < count:
+                stage_da(step - 1)
+            if step in (1, 2):
+                gather(step + 1)
+            if 0 <= step - 2 < count:
+                stage_quant(step - 2)
+                if units[step - 2][1] == HP - 1:
+                    stage_dx(step - 2)
+        nc.sync.dma_start(out, result[:])

@@ -42,23 +42,18 @@ def tile_moe_bdx_glu_sigmoid_kernel(
         w2s = [keep.tile([P, NP * H], U8, name="w2s%d" % e, align_bytes=64) for e in range(E)]
         w13s = keep.tile([P, 2 * E * HP * K], U8, name="w13s", align_bytes=64)
         nc.vector.memset(dys[:].bitcast(I32), 0)
-        for e in range(E):
-            nc.vector.memset(w2s[e][:].bitcast(I32), 0)
-        nc.vector.memset(w13s[:].bitcast(I32), 0)
-
-        warm = keep.tile([P, 1], F32, name="warm")
-        nc.vector.memset(warm[:], 0.0)
-        warm2 = keep.tile([P, 1], F32, name="warm2")
-        nc.scalar.activation(warm2[:], warm[:], SIGMOID)
+        nc.vector.memset(w2s[0][:].bitcast(I32), 0)
 
         ident = keep.tile([P, P], F32, name="ident")
         make_identity(nc, ident[:])
+        warm = keep.tile([P, 1], F32, name="warm")
+        nc.scalar.activation(warm[:], ident[:, 0:1], SIGMOID)
         result = keep.tile([P, T], F32, name="result")
+        nc.gpsimd.memset(w2s[1][:].bitcast(I32), 0)
+        nc.gpsimd.memset(w13s[:].bitcast(I32), 0)
         nc.gpsimd.memset(result[:], 0.0)
 
         gate_col = keep.tile([P, JT], F32, name="gate_col")
-        with nc.allow_non_contiguous_dma(reason="one gate a slot, slots on the partitions"):
-            nc.scalar.dma_start(gate_col[:], gate[0, :].rearrange("(j p) -> p j", p=P))
 
         def load_scales(plane, src, blocks):
             rows = src.rearrange("b (q r) n -> r q b n", r=4)
@@ -67,10 +62,10 @@ def tile_moe_bdx_glu_sigmoid_kernel(
                     plane[r:P:32, :].bitcast(I32).rearrange("q (b n) -> q b n", b=blocks), rows[r].bitcast(I32)
                 )
 
-        dyw = [keep.tile([P, T], U32, name="dyw%d" % o, align_bytes=64) for o in range(NP)]
-
-        def load_dy(o):
-            nc.sync.dma_start(dyw[o][:].bitcast(I32), dy_words[o].rearrange("p t d -> p (t d)").bitcast(I32))
+        dy_first = keep.tile([P, T], U32, name="dy_first", align_bytes=64)
+        dy_rest = keep.tile([P, NP - 1, T], U32, name="dy_rest", align_bytes=64)
+        dyw = [dy_first[:]] + [dy_rest[:, o, :] for o in range(NP - 1)]
+        dy_rows = dy_words.rearrange("o p t d -> p o (t d)").bitcast(I32)
 
         w2w = {}
         a1s = {}
@@ -88,17 +83,18 @@ def tile_moe_bdx_glu_sigmoid_kernel(
 
         w13w = keep.tile([P, 2, E * HP, 2 * K], U8, name="w13w", align_bytes=64)
 
-        load_dy(0)
+        nc.sync.dma_start(dy_first[:].bitcast(I32), dy_rows[:, 0, :])
         load_scales(dys, dy_scales, NP)
-        load_dy(1)
-        load_dy(2)
-        load_scales(w2s[0], w2_scales[0], NP)
+        nc.sync.dma_start(dy_rest[:].bitcast(I32), dy_rows[:, 1:, :])
         for e in range(E):
             for g in range(HP):
-                if (e, g) == (1, 0):
-                    load_scales(w2s[1], w2_scales[1], NP)
-                load_w2(e, g)
                 load_a(a1s, a1, "a1", e, g)
+                if g == 0:
+                    load_scales(w2s[e], w2_scales[e], NP)
+                load_w2(e, g)
+                if (e, g) == (0, 0):
+                    with nc.allow_non_contiguous_dma(reason="one gate a slot, slots on the partitions"):
+                        nc.sync.dma_start(gate_col[:], gate[0, :].rearrange("(j p) -> p j", p=P))
                 load_a(a3s, a3, "a3", e, g)
                 if (e, g) == (0, 1):
                     for m, (words, scales) in enumerate(((w1_words, w1_scales), (w3_words, w3_scales))):
@@ -109,13 +105,13 @@ def tile_moe_bdx_glu_sigmoid_kernel(
         gw = {}
         gs = {}
 
-        def gather(j):
-            gw[j] = keep.tile([P, NP, P], U32, name="gw%d" % j, align_bytes=64)
-            gs[j] = keep.tile([P, NP, P], U8, name="gs%d" % j, align_bytes=64)
-            picks = offsets[:, 8 * j : 8 * (j + 1)]
+        def gather(e):
+            gw[e] = keep.tile([P, NP, C], U32, name="gw%d" % e, align_bytes=64)
+            gs[e] = keep.tile([P, NP, C], U8, name="gs%d" % e, align_bytes=64)
+            picks = offsets[:, C // 16 * e : C // 16 * (e + 1)]
             for o in range(NP):
-                nc.vector.tensor_copy(gw[j][:, o, :], dyw[o][:].indirect(picks))
-                nc.vector.tensor_copy(gs[j][:, o, :], dys[:, T * o : T * (o + 1)].indirect(picks))
+                nc.vector.tensor_copy(gw[e][:, o, :], dyw[o].indirect(picks))
+                nc.vector.tensor_copy(gs[e][:, o, :], dys[:, T * o : T * (o + 1)].indirect(picks))
 
         units = [(e, g, jj) for e in range(E) for g in range(HP) for jj in range(JE)]
         sig_t = {}
@@ -131,22 +127,22 @@ def tile_moe_bdx_glu_sigmoid_kernel(
             a1_t = psum.tile([P, 4, P], F32, name="a1_t")
             for t in range(4):
                 nc.tensor.transpose(a1_t[:, t, :], a1s[e, g][:, t, cols], ident[:])
-            sig_t[u] = work.tile([P, 4, P], F32, name="sig_t")
+            sig_t[u] = work.tile([P, 4, P], F32, name="sig_t", bufs=8)
             nc.scalar.activation(sig_t[u][:], a1_t[:], SIGMOID)
             sig_m = work.tile([P, 4, P], F32, name="sig_m")
             nc.scalar.activation(sig_m[:], a1s[e, g][:, :, cols], SIGMOID, scale=-1.0)
-            wfac[u] = work.tile([P, 4, P], F32, name="wfac", bufs=4)
+            wfac[u] = work.tile([P, 4, P], F32, name="wfac", bufs=8)
             nc.gpsimd.tensor_tensor(wfac[u][:], sig_m[:], a3s[e, g][:, :, cols], MULT)
 
         def stage_dh(u):
             e, g, jj = units[u]
             j = JE * e + jj
-            dh_t = psum.tile([P, KP], F32, name="dh_t")
+            dh_t = psum.tile([P, KP], F32, name="dh_t", bufs=3)
             for o in range(NP):
                 nc.tensor.matmul_mx(
                     out=dh_t[:],
-                    lhsT=gw[j][:, o, :].bitcast(FP8X4),
-                    lhsT_scale=gs[j][:, o, :],
+                    lhsT=gw[e][:, o, P * jj : P * (jj + 1)].bitcast(FP8X4),
+                    lhsT_scale=gs[e][:, o, P * jj : P * (jj + 1)],
                     rhs=w2w[e, g][:, o, :].bitcast(FP4X4),
                     rhs_scale=w2s[e][:, H * o + KP * g : H * o + KP * (g + 1)],
                     start=(o == 0),
@@ -158,7 +154,7 @@ def tile_moe_bdx_glu_sigmoid_kernel(
             )
 
         def stage_da(u):
-            t3 = psum.tile([P, 4, P], F32, name="t3", bufs=3)
+            t3 = psum.tile([P, 4, P], F32, name="t3", bufs=2)
             for t in range(4):
                 nc.tensor.transpose(t3[:, t, :], t3_t[u][:, t, :], ident[:])
             da[u] = work.tile([P, 2, P, 4], BF16, name="da", align_bytes=64)
@@ -209,8 +205,6 @@ def tile_moe_bdx_glu_sigmoid_kernel(
                 stage_dh(step)
             if 0 <= step - 1 < count:
                 stage_da(step - 1)
-            if step in (1, 2):
-                gather(step + 1)
             if 0 <= step - 2 < count:
                 stage_quant(step - 2)
                 if units[step - 2][1] == HP - 1:

@@ -5,7 +5,7 @@ from concourse.masks import make_identity
 
 K, T, E, C, H, N = 128, 768, 2, 256, 1024, 1536
 FLOPS = 2 * E * C * H * (N + 2 * K)
-BYTES = N * T + N * T // 32 + 2 * 4 * H * E * C + E * H * (N + 2 * K) * 17 // 32 + 4 * E * C + 128 * 64 + 4 * K * T
+BYTES = N * T * 33 // 32 + 2 * 4 * H * E * C + E * H * (N + 2 * K) * 17 // 32 + 4 * E * C + 128 * 64 + 4 * K * T
 
 F32 = mybir.dt.float32
 BF16 = mybir.dt.bfloat16
@@ -19,11 +19,15 @@ MULT = mybir.AluOpType.mult
 SIGMOID = mybir.ActivationFunctionType.Sigmoid
 
 P = 128
-KP = 512
-NP = N // KP
-HP = H // KP
-JT = E * C // P
-JE = C // P
+PACK = 4
+PASS = P * PACK
+N_PASSES = N // PASS
+H_PASSES = H // PASS
+SLOTS = E * C
+SLOT_TILES = SLOTS // P
+TILES_PER_EXPERT = C // P
+UNITS = H_PASSES * SLOT_TILES
+LIST_ROWS = 16
 
 
 def tile_moe_bdx_glu_sigmoid_kernel(
@@ -32,181 +36,169 @@ def tile_moe_bdx_glu_sigmoid_kernel(
     nc = tc.nc
     with ExitStack() as ctx:
         keep = ctx.enter_context(tc.tile_pool(name="keep", bufs=1))
-        work = ctx.enter_context(tc.tile_pool(name="work", bufs=3))
+        work = ctx.enter_context(tc.tile_pool(name="work", bufs=4))
         psum = ctx.enter_context(tc.psum_pool(name="psum", bufs=2))
 
-        offsets = keep.tile([P, E * C // 16], U16, name="offsets")
+        offsets = keep.tile([P, SLOTS // LIST_ROWS], U16, name="offsets")
         nc.sync.dma_start(offsets[:], offs)
 
-        dys = keep.tile([P, NP * T], U8, name="dys", align_bytes=64)
-        w2s = [keep.tile([P, NP * H], U8, name="w2s%d" % e, align_bytes=64) for e in range(E)]
-        w13s = keep.tile([P, 2 * E * HP * K], U8, name="w13s", align_bytes=64)
-        nc.vector.memset(dys[:].bitcast(I32), 0)
-        nc.vector.memset(w2s[0][:].bitcast(I32), 0)
+        dy_sc = keep.tile([P, N_PASSES * T], U8, name="dy_sc", align_bytes=64)
+        w2_sc = keep.tile([P, E * N_PASSES * H], U8, name="w2_sc", align_bytes=64)
+        w13_sc = keep.tile([P, 2, E * H_PASSES * K], U8, name="w13_sc", align_bytes=64)
+        nc.gpsimd.memset(dy_sc[:].bitcast(I32), 0)
+        nc.vector.memset(w2_sc[:].bitcast(I32), 0)
 
         ident = keep.tile([P, P], F32, name="ident")
         make_identity(nc, ident[:])
         warm = keep.tile([P, 1], F32, name="warm")
         nc.scalar.activation(warm[:], ident[:, 0:1], SIGMOID)
+        nc.gpsimd.memset(w13_sc[:].bitcast(I32), 0)
         result = keep.tile([P, T], F32, name="result")
-        nc.gpsimd.memset(w2s[1][:].bitcast(I32), 0)
-        nc.gpsimd.memset(w13s[:].bitcast(I32), 0)
         nc.gpsimd.memset(result[:], 0.0)
 
-        gate_col = keep.tile([P, JT], F32, name="gate_col")
-
-        def load_scales(plane, src, blocks):
-            rows = src.rearrange("b (q r) n -> r q b n", r=4)
+        def load_scales(tile, src):
+            rows = src.rearrange("s (q r) n -> r q s n", r=4)
             for r in range(4):
-                nc.sync.dma_start(
-                    plane[r:P:32, :].bitcast(I32).rearrange("q (b n) -> q b n", b=blocks), rows[r].bitcast(I32)
-                )
-
-        dy_first = keep.tile([P, T], U32, name="dy_first", align_bytes=64)
-        dy_rest = keep.tile([P, NP - 1, T], U32, name="dy_rest", align_bytes=64)
-        dyw = [dy_first[:]] + [dy_rest[:, o, :] for o in range(NP - 1)]
-        dy_rows = dy_words.rearrange("o p t d -> p o (t d)").bitcast(I32)
-
-        w2w = {}
-        a1s = {}
-        a3s = {}
+                dst = tile[r:P:32, :].bitcast(I32).rearrange("q (s n) -> q s n", s=src.shape[0])
+                nc.sync.dma_start(dst, rows[r].bitcast(I32))
 
         def load_w2(e, g):
-            w2w[e, g] = keep.tile([P, NP, 2 * KP], U8, name="w2w%d%d" % (e, g), align_bytes=64)
-            src = w2_words[e, :, :, 2 * KP * g : 2 * KP * (g + 1)].rearrange("s p b -> p s b")
-            nc.sync.dma_start(w2w[e, g][:].bitcast(I32), src.bitcast(I32))
+            tile = keep.tile([P, N_PASSES, 2 * PASS], U8, name="w2_w%d%d" % (e, g), align_bytes=64)
+            src = w2_words[e, :, :, 2 * PASS * g : 2 * PASS * (g + 1)].rearrange("s p b -> p s b")
+            nc.sync.dma_start(tile[:].bitcast(I32), src.bitcast(I32))
+            return tile
 
-        def load_a(store, src, name, e, g):
-            store[e, g] = keep.tile([P, 4, C], F32, name="%s_%d%d" % (name, e, g))
-            rows = src[KP * g : KP * (g + 1), C * e : C * (e + 1)].rearrange("(p t) c -> p t c", t=4)
-            nc.sync.dma_start(store[e, g][:], rows)
+        def load_saved(src, name, g):
+            tile = keep.tile([P, PACK, SLOTS], F32, name="%s_%d" % (name, g))
+            nc.sync.dma_start(tile[:], src[PASS * g : PASS * (g + 1), :].rearrange("(p t) c -> p t c", t=PACK))
+            return tile
 
-        w13w = keep.tile([P, 2, E * HP, 2 * K], U8, name="w13w", align_bytes=64)
-
+        dy_rows = dy_words.rearrange("o p t d -> p o (t d)").bitcast(I32)
+        dy_first = keep.tile([P, T], U32, name="dy_first", align_bytes=64)
+        dy_rest = keep.tile([P, N_PASSES - 1, T], U32, name="dy_rest", align_bytes=64)
         nc.sync.dma_start(dy_first[:].bitcast(I32), dy_rows[:, 0, :])
-        load_scales(dys, dy_scales, NP)
         nc.sync.dma_start(dy_rest[:].bitcast(I32), dy_rows[:, 1:, :])
+        dy_w = [dy_first[:]] + [dy_rest[:, o, :] for o in range(N_PASSES - 1)]
+        load_scales(dy_sc[:], dy_scales)
+        a1_sb = [load_saved(a1, "a1", 0)]
+        load_scales(w2_sc[:], w2_scales.rearrange("e s f i -> (e s) f i"))
+        w2_w = {(0, 0): load_w2(0, 0)}
+        gate_col = keep.tile([P, SLOT_TILES], F32, name="gate_col")
+        with nc.allow_non_contiguous_dma(reason="one gate a slot, slots on the partitions"):
+            nc.sync.dma_start(gate_col[:], gate[0, :].rearrange("(j p) -> p j", p=P))
+        a3_sb = [load_saved(a3, "a3", 0)]
+        w2_w[1, 0] = load_w2(1, 0)
+        a1_sb.append(load_saved(a1, "a1", 1))
+        w2_w[0, 1] = load_w2(0, 1)
+        a3_sb.append(load_saved(a3, "a3", 1))
+        w2_w[1, 1] = load_w2(1, 1)
+        w13_w = keep.tile([P, 2, E * H_PASSES, 2 * K], U8, name="w13_w", align_bytes=64)
+        for m, (words, scales) in enumerate(((w1_words, w1_scales), (w3_words, w3_scales))):
+            nc.sync.dma_start(w13_w[:, m].bitcast(I32), words.rearrange("e s p b -> p (e s) b").bitcast(I32))
+            load_scales(w13_sc[:, m, :], scales.rearrange("e s f k -> (e s) f k"))
+
+        g_w = []
+        g_sc = []
         for e in range(E):
-            for g in range(HP):
-                load_a(a1s, a1, "a1", e, g)
-                if g == 0:
-                    load_scales(w2s[e], w2_scales[e], NP)
-                load_w2(e, g)
-                if (e, g) == (0, 0):
-                    with nc.allow_non_contiguous_dma(reason="one gate a slot, slots on the partitions"):
-                        nc.sync.dma_start(gate_col[:], gate[0, :].rearrange("(j p) -> p j", p=P))
-                load_a(a3s, a3, "a3", e, g)
-                if (e, g) == (0, 1):
-                    for m, (words, scales) in enumerate(((w1_words, w1_scales), (w3_words, w3_scales))):
-                        nc.sync.dma_start(w13w[:, m].bitcast(I32), words.rearrange("e s p b -> p (e s) b").bitcast(I32))
-                        half = E * HP * K
-                        load_scales(w13s[:, m * half : (m + 1) * half], scales.rearrange("e s f k -> (e s) f k"), E * HP)
+            g_w.append(keep.tile([P, N_PASSES, C], U32, name="g_w%d" % e, align_bytes=64))
+            g_sc.append(keep.tile([P, N_PASSES, C], U8, name="g_sc%d" % e, align_bytes=64))
+            picks = offsets[:, C // LIST_ROWS * e : C // LIST_ROWS * (e + 1)]
+            for o in range(N_PASSES):
+                nc.vector.tensor_copy(g_w[e][:, o, :], dy_w[o].indirect(picks))
+            for o in range(N_PASSES):
+                nc.vector.tensor_copy(g_sc[e][:, o, :], dy_sc[:, T * o : T * (o + 1)].indirect(picks))
 
-        gw = {}
-        gs = {}
-
-        def gather(e):
-            gw[e] = keep.tile([P, NP, C], U32, name="gw%d" % e, align_bytes=64)
-            gs[e] = keep.tile([P, NP, C], U8, name="gs%d" % e, align_bytes=64)
-            picks = offsets[:, C // 16 * e : C // 16 * (e + 1)]
-            for o in range(NP):
-                nc.vector.tensor_copy(gw[e][:, o, :], dyw[o].indirect(picks))
-                nc.vector.tensor_copy(gs[e][:, o, :], dys[:, T * o : T * (o + 1)].indirect(picks))
-
-        units = [(e, g, jj) for e in range(E) for g in range(HP) for jj in range(JE)]
         sig_t = {}
-        wfac = {}
-        t3_t = {}
+        a3_rest = {}
+        da3_t = {}
         da = {}
-        codes = {}
-        cscales = {}
+        da_w = {}
+        da_sc = {}
 
-        def stage_sigmoid(u):
-            e, g, jj = units[u]
-            cols = slice(P * jj, P * (jj + 1))
-            a1_t = psum.tile([P, 4, P], F32, name="a1_t")
-            for t in range(4):
-                nc.tensor.transpose(a1_t[:, t, :], a1s[e, g][:, t, cols], ident[:])
-            sig_t[u] = work.tile([P, 4, P], F32, name="sig_t", bufs=8)
+        def sigmoids(u):
+            g, j = divmod(u, SLOT_TILES)
+            slots = slice(P * j, P * (j + 1))
+            a1_t = psum.tile([P, PACK, P], F32, name="a1_t")
+            for t in range(PACK):
+                nc.tensor.transpose(a1_t[:, t, :], a1_sb[g][:, t, slots], ident[:])
+            sig_t[u] = keep.tile([P, PACK, P], F32, name="sig_t%d" % u)
             nc.scalar.activation(sig_t[u][:], a1_t[:], SIGMOID)
-            sig_m = work.tile([P, 4, P], F32, name="sig_m")
-            nc.scalar.activation(sig_m[:], a1s[e, g][:, :, cols], SIGMOID, scale=-1.0)
-            wfac[u] = work.tile([P, 4, P], F32, name="wfac", bufs=8)
-            nc.gpsimd.tensor_tensor(wfac[u][:], sig_m[:], a3s[e, g][:, :, cols], MULT)
+            rest = keep.tile([P, PACK, P], F32, name="rest%d" % u)
+            nc.scalar.activation(rest[:], a1_sb[g][:, :, slots], SIGMOID, scale=-1.0)
+            a3_rest[u] = keep.tile([P, PACK, P], F32, name="a3_rest%d" % u)
+            nc.gpsimd.tensor_tensor(a3_rest[u][:], rest[:], a3_sb[g][:, :, slots], MULT)
 
-        def stage_dh(u):
-            e, g, jj = units[u]
-            j = JE * e + jj
-            dh_t = psum.tile([P, KP], F32, name="dh_t", bufs=3)
-            for o in range(NP):
+        def first_product(u):
+            g, j = divmod(u, SLOT_TILES)
+            e, jj = divmod(j, TILES_PER_EXPERT)
+            sums = psum.tile([P, PASS], F32, name="sums", bufs=2)
+            for o in range(N_PASSES):
+                first = H * (N_PASSES * e + o) + PASS * g
                 nc.tensor.matmul_mx(
-                    out=dh_t[:],
-                    lhsT=gw[e][:, o, P * jj : P * (jj + 1)].bitcast(FP8X4),
-                    lhsT_scale=gs[e][:, o, P * jj : P * (jj + 1)],
-                    rhs=w2w[e, g][:, o, :].bitcast(FP4X4),
-                    rhs_scale=w2s[e][:, H * o + KP * g : H * o + KP * (g + 1)],
+                    out=sums[:],
+                    lhsT=g_w[e][:, o, P * jj : P * (jj + 1)].bitcast(FP8X4),
+                    lhsT_scale=g_sc[e][:, o, P * jj : P * (jj + 1)],
+                    rhs=w2_w[e, g][:, o, :].bitcast(FP4X4),
+                    rhs_scale=w2_sc[:, first : first + PASS],
                     start=(o == 0),
-                    stop=(o == NP - 1),
+                    stop=(o == N_PASSES - 1),
                 )
-            t3_t[u] = work.tile([P, 4, P], F32, name="t3_t")
+            da3_t[u] = work.tile([P, PACK, P], F32, name="da3_t")
             nc.vector.scalar_tensor_tensor(
-                t3_t[u][:], dh_t[:].rearrange("p (m t) -> p t m", t=4), gate_col[:, j : j + 1], sig_t[u][:], MULT, MULT
+                da3_t[u][:], sums[:].rearrange("n (p t) -> n t p", t=PACK), gate_col[:, j : j + 1], sig_t[u][:], MULT, MULT
             )
 
-        def stage_da(u):
-            t3 = psum.tile([P, 4, P], F32, name="t3", bufs=2)
-            for t in range(4):
-                nc.tensor.transpose(t3[:, t, :], t3_t[u][:, t, :], ident[:])
-            da[u] = work.tile([P, 2, P, 4], BF16, name="da", align_bytes=64)
+        def turn_and_round(u):
+            da3 = psum.tile([P, PACK, P], F32, name="da3", bufs=3)
+            for t in range(PACK):
+                nc.tensor.transpose(da3[:, t, :], da3_t[u][:, t, :], ident[:])
+            da[u] = work.tile([P, 2, P, PACK], BF16, name="da", align_bytes=64)
             nc.vector.tensor_tensor(
-                da[u][:, 0].rearrange("p (c i) t -> p c t i", i=4),
-                t3[:].rearrange("p t (c i) -> p c t i", i=4),
-                wfac[u][:].rearrange("p t (c i) -> p c t i", i=4),
+                da[u][:, 0].rearrange("p (c x) t -> p c t x", x=4),
+                da3[:].rearrange("p t (c x) -> p c t x", x=4),
+                a3_rest[u][:].rearrange("p t (c x) -> p c t x", x=4),
                 MULT,
             )
-            nc.scalar.copy(da[u][:, 1], t3[:].rearrange("p t n -> p n t"))
+            nc.scalar.copy(da[u][:, 1], da3[:].rearrange("p t n -> p n t"))
 
-        def stage_quant(u):
-            codes[u] = keep.tile([P, 2 * P], U32, name="codes%d" % u, align_bytes=64)
-            cscales[u] = keep.tile([P, 2 * P], U8, name="cscales%d" % u, align_bytes=64)
+        def quantise(u):
+            da_w[u] = keep.tile([P, 2 * P], U32, name="da_w%d" % u, align_bytes=64)
+            da_sc[u] = keep.tile([P, 2 * P], U8, name="da_sc%d" % u, align_bytes=64)
             nc.vector.quantize_mx(
-                out=codes[u][:].bitcast(FP8X4), scales=cscales[u][:], in_=da[u][:].rearrange("p m n t -> p (m n t)")
+                out=da_w[u][:].bitcast(FP8X4), scales=da_sc[u][:], in_=da[u][:].rearrange("p m n t -> p (m n t)")
             )
 
-        def stage_dx(u):
-            e, g, jj = units[u]
-            j = JE * e + jj
+        def second_product(j):
+            e = j // TILES_PER_EXPERT
             dx = psum.tile([P, P], F32, name="dx", bufs=1)
-            for gg in range(HP):
-                v = units.index((e, gg, jj))
+            for g in range(H_PASSES):
+                u = SLOT_TILES * g + j
+                s = H_PASSES * e + g
                 for m in range(2):
-                    blk = (m * E + e) * HP + gg
                     nc.tensor.matmul_mx(
                         out=dx[:],
-                        lhsT=w13w[:, m, e * HP + gg, :].bitcast(FP4X4),
-                        lhsT_scale=w13s[:, K * blk : K * (blk + 1)],
-                        rhs=codes[v][:, P * m : P * (m + 1)].bitcast(FP8X4),
-                        rhs_scale=cscales[v][:, P * m : P * (m + 1)],
-                        start=(gg == 0 and m == 0),
-                        stop=(gg == HP - 1 and m == 1),
+                        lhsT=w13_w[:, m, s, :].bitcast(FP4X4),
+                        lhsT_scale=w13_sc[:, m, K * s : K * (s + 1)],
+                        rhs=da_w[u][:, P * m : P * (m + 1)].bitcast(FP8X4),
+                        rhs_scale=da_sc[u][:, P * m : P * (m + 1)],
+                        start=(g == 0 and m == 0),
+                        stop=(g == H_PASSES - 1 and m == 1),
                     )
             dx_sb = work.tile([P, P], F32, name="dx_sb")
             nc.scalar.copy(dx_sb[:], dx[:])
-            nc.vector.tensor_copy(result[:].indirect(offsets[:, 8 * j : 8 * (j + 1)]), dx_sb[:])
+            places = offsets[:, P // LIST_ROWS * j : P // LIST_ROWS * (j + 1)]
+            nc.vector.tensor_copy(result[:].indirect(places), dx_sb[:])
 
-        gather(0)
-        gather(1)
-        stage_sigmoid(0)
-        count = len(units)
-        for step in range(count + 2):
-            if step + 1 < count:
-                stage_sigmoid(step + 1)
-            if step < count:
-                stage_dh(step)
-            if 0 <= step - 1 < count:
-                stage_da(step - 1)
-            if 0 <= step - 2 < count:
-                stage_quant(step - 2)
-                if units[step - 2][1] == HP - 1:
-                    stage_dx(step - 2)
+        sigmoids(0)
+        for step in range(UNITS + 2):
+            if step + 1 < UNITS:
+                sigmoids(step + 1)
+            if step < UNITS:
+                first_product(step)
+            if 1 <= step <= UNITS:
+                turn_and_round(step - 1)
+            if step >= 2:
+                quantise(step - 2)
+                if step - 2 >= UNITS - SLOT_TILES:
+                    second_product((step - 2) % SLOT_TILES)
         nc.sync.dma_start(out, result[:])

@@ -154,9 +154,9 @@ def tile_moe_bdx_glu_sigmoid_kernel(
                 nc.tensor.transpose(da3[:, t, :], da3_t[u][:, t, :], ident[:])
             da[u] = work.tile([P, 2, P, PACK], BF16, name="da", align_bytes=64)
             nc.vector.tensor_tensor(
-                da[u][:, 0].rearrange("p (c x) t -> p c t x", x=4),
-                da3[:].rearrange("p t (c x) -> p c t x", x=4),
-                a3_rest[u][:].rearrange("p t (c x) -> p c t x", x=4),
+                da[u][:, 0].rearrange("p (c x) t -> p c t x", x=2),
+                da3[:].rearrange("p t (c x) -> p c t x", x=2),
+                a3_rest[u][:].rearrange("p t (c x) -> p c t x", x=2),
                 MULT,
             )
             nc.scalar.copy(da[u][:, 1], da3[:].rearrange("p t n -> p n t"))

@@ -5,7 +5,7 @@ from concourse.masks import make_identity
 
 K, T, E, C, H, N = 128, 768, 2, 256, 1024, 1536
 FLOPS = 2 * E * C * H * (N + 2 * K)
-BYTES = N * T * 33 // 32 + 2 * 4 * H * E * C + E * H * (N + 2 * K) * 17 // 32 + 4 * E * C + 128 * 64 + 4 * K * T
+BYTES = N * T * 33 // 32 + 2 * 4 * H * E * C + E * H * (N + 2 * K) * 17 // 32 + 4 * E * C + 16 * E * C + 4 * K * T
 
 F32 = mybir.dt.float32
 BF16 = mybir.dt.bfloat16
@@ -16,6 +16,8 @@ U8 = mybir.dt.uint8
 FP8X4 = mybir.dt.float8_e4m3fn_x4
 FP4X4 = mybir.dt.float4_e2m1fn_x4
 MULT = mybir.AluOpType.mult
+SUBTRACT = mybir.AluOpType.subtract
+COPY = mybir.ActivationFunctionType.Copy
 SIGMOID = mybir.ActivationFunctionType.Sigmoid
 
 P = 128
@@ -37,7 +39,7 @@ def tile_moe_bdx_glu_sigmoid_kernel(
     with ExitStack() as ctx:
         keep = ctx.enter_context(tc.tile_pool(name="keep", bufs=1))
         work = ctx.enter_context(tc.tile_pool(name="work", bufs=4))
-        psum = ctx.enter_context(tc.psum_pool(name="psum", bufs=2))
+        psum = ctx.enter_context(tc.psum_pool(name="psum", bufs=3))
 
         offsets = keep.tile([P, SLOTS // LIST_ROWS], U16, name="offsets")
         nc.sync.dma_start(offsets[:], offs)
@@ -50,8 +52,6 @@ def tile_moe_bdx_glu_sigmoid_kernel(
 
         ident = keep.tile([P, P], F32, name="ident")
         make_identity(nc, ident[:])
-        warm = keep.tile([P, 1], F32, name="warm")
-        nc.scalar.activation(warm[:], ident[:, 0:1], SIGMOID)
         nc.gpsimd.memset(w13_sc[:].bitcast(I32), 0)
         result = keep.tile([P, T], F32, name="result")
         nc.gpsimd.memset(result[:], 0.0)
@@ -68,9 +68,10 @@ def tile_moe_bdx_glu_sigmoid_kernel(
             nc.sync.dma_start(tile[:].bitcast(I32), src.bitcast(I32))
             return tile
 
-        def load_saved(src, name, g):
-            tile = keep.tile([P, PACK, SLOTS], F32, name="%s_%d" % (name, g))
-            nc.sync.dma_start(tile[:], src[PASS * g : PASS * (g + 1), :].rearrange("(p t) c -> p t c", t=PACK))
+        def load_saved(src, name, e, g):
+            tile = keep.tile([P, PACK, C], F32, name="%s_%d%d" % (name, e, g))
+            rows = src[PASS * g : PASS * (g + 1), C * e : C * (e + 1)]
+            nc.sync.dma_start(tile[:], rows.rearrange("(p t) c -> p t c", t=PACK))
             return tile
 
         dy_rows = dy_words.rearrange("o p t d -> p o (t d)").bitcast(I32)
@@ -80,18 +81,23 @@ def tile_moe_bdx_glu_sigmoid_kernel(
         nc.sync.dma_start(dy_rest[:].bitcast(I32), dy_rows[:, 1:, :])
         dy_w = [dy_first[:]] + [dy_rest[:, o, :] for o in range(N_PASSES - 1)]
         load_scales(dy_sc[:], dy_scales)
-        a1_sb = [load_saved(a1, "a1", 0)]
-        load_scales(w2_sc[:], w2_scales.rearrange("e s f i -> (e s) f i"))
-        w2_w = {(0, 0): load_w2(0, 0)}
+        w2_w = {}
+        a1_sb = {}
+        a3_sb = {}
         gate_col = keep.tile([P, SLOT_TILES], F32, name="gate_col")
-        with nc.allow_non_contiguous_dma(reason="one gate a slot, slots on the partitions"):
-            nc.sync.dma_start(gate_col[:], gate[0, :].rearrange("(j p) -> p j", p=P))
-        a3_sb = [load_saved(a3, "a3", 0)]
-        w2_w[1, 0] = load_w2(1, 0)
-        a1_sb.append(load_saved(a1, "a1", 1))
-        w2_w[0, 1] = load_w2(0, 1)
-        a3_sb.append(load_saved(a3, "a3", 1))
-        w2_w[1, 1] = load_w2(1, 1)
+        for g in range(H_PASSES):
+            for e in range(E):
+                first_unit = (e, g) == (0, 0)
+                a1_sb[e, g] = load_saved(a1, "a1", e, g)
+                if first_unit:
+                    load_scales(w2_sc[:], w2_scales.rearrange("e s f i -> (e s) f i"))
+                w2_w[e, g] = load_w2(e, g)
+                if first_unit:
+                    with nc.allow_non_contiguous_dma(reason="one gate a slot, slots on the partitions"):
+                        nc.sync.dma_start(gate_col[:], gate[0, :].rearrange("(j p) -> p j", p=P))
+                a3_sb[e, g] = load_saved(a3, "a3", e, g)
+        neg_gate = keep.tile([P, SLOT_TILES], F32, name="neg_gate")
+        nc.vector.tensor_scalar_mul(neg_gate[:], gate_col[:], -1.0)
         w13_w = keep.tile([P, 2, E * H_PASSES, 2 * K], U8, name="w13_w", align_bytes=64)
         for m, (words, scales) in enumerate(((w1_words, w1_scales), (w3_words, w3_scales))):
             nc.sync.dma_start(w13_w[:, m].bitcast(I32), words.rearrange("e s p b -> p (e s) b").bitcast(I32))
@@ -108,30 +114,26 @@ def tile_moe_bdx_glu_sigmoid_kernel(
             for o in range(N_PASSES):
                 nc.vector.tensor_copy(g_sc[e][:, o, :], dy_sc[:, T * o : T * (o + 1)].indirect(picks))
 
-        sig_t = {}
-        a3_rest = {}
-        da3_t = {}
+        sig = {}
+        neg_factor = {}
+        neg_dh_t = {}
         da = {}
         da_w = {}
         da_sc = {}
 
-        def sigmoids(u):
+        def factors(u):
             g, j = divmod(u, SLOT_TILES)
-            slots = slice(P * j, P * (j + 1))
-            a1_t = psum.tile([P, PACK, P], F32, name="a1_t")
-            for t in range(PACK):
-                nc.tensor.transpose(a1_t[:, t, :], a1_sb[g][:, t, slots], ident[:])
-            sig_t[u] = keep.tile([P, PACK, P], F32, name="sig_t%d" % u)
-            nc.scalar.activation(sig_t[u][:], a1_t[:], SIGMOID)
-            rest = keep.tile([P, PACK, P], F32, name="rest%d" % u)
-            nc.scalar.activation(rest[:], a1_sb[g][:, :, slots], SIGMOID, scale=-1.0)
-            a3_rest[u] = keep.tile([P, PACK, P], F32, name="a3_rest%d" % u)
-            nc.gpsimd.tensor_tensor(a3_rest[u][:], rest[:], a3_sb[g][:, :, slots], MULT)
+            e, jj = divmod(j, TILES_PER_EXPERT)
+            places = slice(P * jj, P * (jj + 1))
+            sig[u] = keep.tile([P, PACK, P], F32, name="sig%d" % u)
+            nc.scalar.activation(sig[u][:], a1_sb[e, g][:, :, places], SIGMOID)
+            neg_factor[u] = keep.tile([P, PACK, P], F32, name="neg_factor%d" % u)
+            nc.vector.scalar_tensor_tensor(neg_factor[u][:], sig[u][:], 1.0, a3_sb[e, g][:, :, places], SUBTRACT, MULT)
 
         def first_product(u):
             g, j = divmod(u, SLOT_TILES)
             e, jj = divmod(j, TILES_PER_EXPERT)
-            sums = psum.tile([P, PASS], F32, name="sums", bufs=2)
+            sums = psum.tile([P, PASS], F32, name="sums")
             for o in range(N_PASSES):
                 first = H * (N_PASSES * e + o) + PASS * g
                 nc.tensor.matmul_mx(
@@ -143,23 +145,25 @@ def tile_moe_bdx_glu_sigmoid_kernel(
                     start=(o == 0),
                     stop=(o == N_PASSES - 1),
                 )
-            da3_t[u] = work.tile([P, PACK, P], F32, name="da3_t")
-            nc.vector.scalar_tensor_tensor(
-                da3_t[u][:], sums[:].rearrange("n (p t) -> n t p", t=PACK), gate_col[:, j : j + 1], sig_t[u][:], MULT, MULT
+            neg_dh_t[u] = work.tile([P, PACK, P], F32, name="neg_dh_t")
+            nc.scalar.activation(
+                neg_dh_t[u][:], sums[:].rearrange("n (p t) -> n t p", t=PACK), COPY, scale=neg_gate[:, j : j + 1]
             )
 
         def turn_and_round(u):
-            da3 = psum.tile([P, PACK, P], F32, name="da3", bufs=3)
+            neg_dh = psum.tile([P, PACK, P], F32, name="neg_dh")
             for t in range(PACK):
-                nc.tensor.transpose(da3[:, t, :], da3_t[u][:, t, :], ident[:])
+                nc.tensor.transpose(neg_dh[:, t, :], neg_dh_t[u][:, t, :], ident[:])
+            neg_da3 = work.tile([P, PACK, P], F32, name="neg_da3")
+            nc.vector.tensor_tensor(neg_da3[:], neg_dh[:], sig[u][:], MULT)
             da[u] = work.tile([P, 2, P, PACK], BF16, name="da", align_bytes=64)
             nc.vector.tensor_tensor(
                 da[u][:, 0].rearrange("p (c x) t -> p c t x", x=2),
-                da3[:].rearrange("p t (c x) -> p c t x", x=2),
-                a3_rest[u][:].rearrange("p t (c x) -> p c t x", x=2),
+                neg_da3[:].rearrange("p t (c x) -> p c t x", x=2),
+                neg_factor[u][:].rearrange("p t (c x) -> p c t x", x=2),
                 MULT,
             )
-            nc.scalar.copy(da[u][:, 1], da3[:].rearrange("p t n -> p n t"))
+            nc.scalar.activation(da[u][:, 1], neg_da3[:].rearrange("p t n -> p n t"), COPY, scale=-1.0)
 
         def quantise(u):
             da_w[u] = keep.tile([P, 2 * P], U32, name="da_w%d" % u, align_bytes=64)
@@ -186,13 +190,13 @@ def tile_moe_bdx_glu_sigmoid_kernel(
                     )
             dx_sb = work.tile([P, P], F32, name="dx_sb")
             nc.scalar.copy(dx_sb[:], dx[:])
-            places = offsets[:, P // LIST_ROWS * j : P // LIST_ROWS * (j + 1)]
-            nc.vector.tensor_copy(result[:].indirect(places), dx_sb[:])
+            tokens = offsets[:, P // LIST_ROWS * j : P // LIST_ROWS * (j + 1)]
+            nc.vector.tensor_copy(result[:].indirect(tokens), dx_sb[:])
 
-        sigmoids(0)
+        factors(0)
         for step in range(UNITS + 2):
             if step + 1 < UNITS:
-                sigmoids(step + 1)
+                factors(step + 1)
             if step < UNITS:
                 first_product(step)
             if 1 <= step <= UNITS:

from contextlib import ExitStack

import concourse.mybir as mybir
from concourse.masks import make_identity

K, T, E, C, H, N = 128, 768, 2, 256, 1024, 1536
FLOPS = 2 * E * C * H * (N + 2 * K)
BYTES = N * T * 33 // 32 + 2 * 4 * H * E * C + E * H * (N + 2 * K) * 17 // 32 + 4 * E * C + 16 * E * C + 4 * K * T

F32 = mybir.dt.float32
BF16 = mybir.dt.bfloat16
I32 = mybir.dt.int32
U32 = mybir.dt.uint32
U16 = mybir.dt.uint16
U8 = mybir.dt.uint8
FP8X4 = mybir.dt.float8_e4m3fn_x4
FP4X4 = mybir.dt.float4_e2m1fn_x4
MULT = mybir.AluOpType.mult
SUBTRACT = mybir.AluOpType.subtract
COPY = mybir.ActivationFunctionType.Copy
SIGMOID = mybir.ActivationFunctionType.Sigmoid

P = 128
PACK = 4
PASS = P * PACK
N_PASSES = N // PASS
H_PASSES = H // PASS
SLOTS = E * C
SLOT_TILES = SLOTS // P
TILES_PER_EXPERT = C // P
UNITS = H_PASSES * SLOT_TILES
LIST_ROWS = 16


def tile_moe_bdx_glu_sigmoid_kernel(
    tc, dy_words, dy_scales, a1, a3, w2_words, w2_scales, w1_words, w1_scales, w3_words, w3_scales, gate, offs, out
):
    nc = tc.nc
    with ExitStack() as ctx:
        keep = ctx.enter_context(tc.tile_pool(name="keep", bufs=1))
        work = ctx.enter_context(tc.tile_pool(name="work", bufs=4))
        psum = ctx.enter_context(tc.psum_pool(name="psum", bufs=3))

        offsets = keep.tile([P, SLOTS // LIST_ROWS], U16, name="offsets")
        nc.sync.dma_start(offsets[:], offs)

        dy_sc = keep.tile([P, N_PASSES * T], U8, name="dy_sc", align_bytes=64)
        w2_sc = keep.tile([P, E * N_PASSES * H], U8, name="w2_sc", align_bytes=64)
        w13_sc = keep.tile([P, 2, E * H_PASSES * K], U8, name="w13_sc", align_bytes=64)
        nc.gpsimd.memset(dy_sc[:].bitcast(I32), 0)
        nc.vector.memset(w2_sc[:].bitcast(I32), 0)

        ident = keep.tile([P, P], F32, name="ident")
        make_identity(nc, ident[:])
        nc.gpsimd.memset(w13_sc[:].bitcast(I32), 0)
        result = keep.tile([P, T], F32, name="result")
        nc.gpsimd.memset(result[:], 0.0)

        def load_scales(tile, src):
            rows = src.rearrange("s (q r) n -> r q s n", r=4)
            for r in range(4):
                dst = tile[r:P:32, :].bitcast(I32).rearrange("q (s n) -> q s n", s=src.shape[0])
                nc.sync.dma_start(dst, rows[r].bitcast(I32))

        def load_w2(e, g):
            tile = keep.tile([P, N_PASSES, 2 * PASS], U8, name="w2_w%d%d" % (e, g), align_bytes=64)
            src = w2_words[e, :, :, 2 * PASS * g : 2 * PASS * (g + 1)].rearrange("s p b -> p s b")
            nc.sync.dma_start(tile[:].bitcast(I32), src.bitcast(I32))
            return tile

        def load_saved(src, name, e, g):
            tile = keep.tile([P, PACK, C], F32, name="%s_%d%d" % (name, e, g))
            rows = src[PASS * g : PASS * (g + 1), C * e : C * (e + 1)]
            nc.sync.dma_start(tile[:], rows.rearrange("(p t) c -> p t c", t=PACK))
            return tile

        dy_rows = dy_words.rearrange("o p t d -> p o (t d)").bitcast(I32)
        dy_first = keep.tile([P, T], U32, name="dy_first", align_bytes=64)
        dy_rest = keep.tile([P, N_PASSES - 1, T], U32, name="dy_rest", align_bytes=64)
        nc.sync.dma_start(dy_first[:].bitcast(I32), dy_rows[:, 0, :])
        nc.sync.dma_start(dy_rest[:].bitcast(I32), dy_rows[:, 1:, :])
        dy_w = [dy_first[:]] + [dy_rest[:, o, :] for o in range(N_PASSES - 1)]
        load_scales(dy_sc[:], dy_scales)
        w2_w = {}
        a1_sb = {}
        a3_sb = {}
        gate_col = keep.tile([P, SLOT_TILES], F32, name="gate_col")
        for g in range(H_PASSES):
            for e in range(E):
                first_unit = (e, g) == (0, 0)
                a1_sb[e, g] = load_saved(a1, "a1", e, g)
                if first_unit:
                    load_scales(w2_sc[:], w2_scales.rearrange("e s f i -> (e s) f i"))
                w2_w[e, g] = load_w2(e, g)
                if first_unit:
                    with nc.allow_non_contiguous_dma(reason="one gate a slot, slots on the partitions"):
                        nc.sync.dma_start(gate_col[:], gate[0, :].rearrange("(j p) -> p j", p=P))
                a3_sb[e, g] = load_saved(a3, "a3", e, g)
        neg_gate = keep.tile([P, SLOT_TILES], F32, name="neg_gate")
        nc.vector.tensor_scalar_mul(neg_gate[:], gate_col[:], -1.0)
        w13_w = keep.tile([P, 2, E * H_PASSES, 2 * K], U8, name="w13_w", align_bytes=64)
        for m, (words, scales) in enumerate(((w1_words, w1_scales), (w3_words, w3_scales))):
            nc.sync.dma_start(w13_w[:, m].bitcast(I32), words.rearrange("e s p b -> p (e s) b").bitcast(I32))
            load_scales(w13_sc[:, m, :], scales.rearrange("e s f k -> (e s) f k"))

        g_w = []
        g_sc = []
        for e in range(E):
            g_w.append(keep.tile([P, N_PASSES, C], U32, name="g_w%d" % e, align_bytes=64))
            g_sc.append(keep.tile([P, N_PASSES, C], U8, name="g_sc%d" % e, align_bytes=64))
            picks = offsets[:, C // LIST_ROWS * e : C // LIST_ROWS * (e + 1)]
            for o in range(N_PASSES):
                nc.vector.tensor_copy(g_w[e][:, o, :], dy_w[o].indirect(picks))
            for o in range(N_PASSES):
                nc.vector.tensor_copy(g_sc[e][:, o, :], dy_sc[:, T * o : T * (o + 1)].indirect(picks))

        sig = {}
        neg_factor = {}
        neg_dh_t = {}
        da = {}
        da_w = {}
        da_sc = {}

        def factors(u):
            g, j = divmod(u, SLOT_TILES)
            e, jj = divmod(j, TILES_PER_EXPERT)
            places = slice(P * jj, P * (jj + 1))
            sig[u] = keep.tile([P, PACK, P], F32, name="sig%d" % u)
            nc.scalar.activation(sig[u][:], a1_sb[e, g][:, :, places], SIGMOID)
            neg_factor[u] = keep.tile([P, PACK, P], F32, name="neg_factor%d" % u)
            nc.vector.scalar_tensor_tensor(neg_factor[u][:], sig[u][:], 1.0, a3_sb[e, g][:, :, places], SUBTRACT, MULT)

        def first_product(u):
            g, j = divmod(u, SLOT_TILES)
            e, jj = divmod(j, TILES_PER_EXPERT)
            sums = psum.tile([P, PASS], F32, name="sums")
            for o in range(N_PASSES):
                first = H * (N_PASSES * e + o) + PASS * g
                nc.tensor.matmul_mx(
                    out=sums[:],
                    lhsT=g_w[e][:, o, P * jj : P * (jj + 1)].bitcast(FP8X4),
                    lhsT_scale=g_sc[e][:, o, P * jj : P * (jj + 1)],
                    rhs=w2_w[e, g][:, o, :].bitcast(FP4X4),
                    rhs_scale=w2_sc[:, first : first + PASS],
                    start=(o == 0),
                    stop=(o == N_PASSES - 1),
                )
            neg_dh_t[u] = work.tile([P, PACK, P], F32, name="neg_dh_t")
            nc.scalar.activation(
                neg_dh_t[u][:], sums[:].rearrange("n (p t) -> n t p", t=PACK), COPY, scale=neg_gate[:, j : j + 1]
            )

        def turn_and_round(u):
            neg_dh = psum.tile([P, PACK, P], F32, name="neg_dh")
            for t in range(PACK):
                nc.tensor.transpose(neg_dh[:, t, :], neg_dh_t[u][:, t, :], ident[:])
            neg_da3 = work.tile([P, PACK, P], F32, name="neg_da3")
            nc.vector.tensor_tensor(neg_da3[:], neg_dh[:], sig[u][:], MULT)
            da[u] = work.tile([P, 2, P, PACK], BF16, name="da", align_bytes=64)
            nc.vector.tensor_tensor(
                da[u][:, 0].rearrange("p (c x) t -> p c t x", x=2),
                neg_da3[:].rearrange("p t (c x) -> p c t x", x=2),
                neg_factor[u][:].rearrange("p t (c x) -> p c t x", x=2),
                MULT,
            )
            nc.scalar.activation(da[u][:, 1], neg_da3[:].rearrange("p t n -> p n t"), COPY, scale=-1.0)

        def quantise(u):
            da_w[u] = keep.tile([P, 2 * P], U32, name="da_w%d" % u, align_bytes=64)
            da_sc[u] = keep.tile([P, 2 * P], U8, name="da_sc%d" % u, align_bytes=64)
            nc.vector.quantize_mx(
                out=da_w[u][:].bitcast(FP8X4), scales=da_sc[u][:], in_=da[u][:].rearrange("p m n t -> p (m n t)")
            )

        def second_product(j):
            e = j // TILES_PER_EXPERT
            dx = psum.tile([P, P], F32, name="dx", bufs=1)
            for g in range(H_PASSES):
                u = SLOT_TILES * g + j
                s = H_PASSES * e + g
                for m in range(2):
                    nc.tensor.matmul_mx(
                        out=dx[:],
                        lhsT=w13_w[:, m, s, :].bitcast(FP4X4),
                        lhsT_scale=w13_sc[:, m, K * s : K * (s + 1)],
                        rhs=da_w[u][:, P * m : P * (m + 1)].bitcast(FP8X4),
                        rhs_scale=da_sc[u][:, P * m : P * (m + 1)],
                        start=(g == 0 and m == 0),
                        stop=(g == H_PASSES - 1 and m == 1),
                    )
            dx_sb = work.tile([P, P], F32, name="dx_sb")
            nc.scalar.copy(dx_sb[:], dx[:])
            tokens = offsets[:, P // LIST_ROWS * j : P // LIST_ROWS * (j + 1)]
            nc.vector.tensor_copy(result[:].indirect(tokens), dx_sb[:])

        factors(0)
        for step in range(UNITS + 2):
            if step + 1 < UNITS:
                factors(step + 1)
            if step < UNITS:
                first_product(step)
            if 1 <= step <= UNITS:
                turn_and_round(step - 1)
            if step >= 2:
                quantise(step - 2)
                if step - 2 >= UNITS - SLOT_TILES:
                    second_product((step - 2) % SLOT_TILES)
        nc.sync.dma_start(out, result[:])
